import numpy as np
import ml_dtypes


def mxq(x, axis, fmt="e4m3"):
    dtype, down = {"e4m3": (ml_dtypes.float8_e4m3fn, 7), "e5m2": (ml_dtypes.float8_e5m2, 14)}[fmt]
    v = np.moveaxis(np.asarray(x, np.float32).astype(ml_dtypes.bfloat16).astype(np.float64), axis, -1)
    blocks = v.reshape(v.shape[:-1] + (-1, 32))
    amax = np.abs(blocks).max(-1, keepdims=True)
    byte = np.maximum(np.where(amax > 0, np.frexp(amax)[1] - 1 + 127, 0) - down, 1)
    scale = np.exp2(byte - 127.0)
    codes = (blocks / scale).astype(np.float32).astype(dtype).astype(np.float64)
    return np.moveaxis((codes * scale).reshape(v.shape), -1, axis)


WIDE = False


def mx_kscale(k):
    if not WIDE:
        return np.ones(k)
    levels = np.array([10, -10, 5, -5, 0])
    if k % 512:
        return np.exp2(np.random.permutation(np.resize(levels, k // 32))).repeat(32)
    a = np.empty((k // 512, 16))
    for p in range(k // 512):
        a[p, :8] = np.random.permutation(np.resize(levels, 8))
        for g in range(8):
            far = levels[np.abs(levels - a[p, g]) >= 10]
            a[p, g + 8] = far[np.random.randint(len(far))]
    return np.exp2(a.ravel()).repeat(32)


def f64(x):
    return np.asarray(x).astype(np.float64)


def striped(idx):
    return np.tile(idx.reshape(-1, 16).T, (8, 1)).astype(np.uint16)


def unstriped(offs):
    return offs[:16].T.reshape(-1).astype(np.int64)


E2M1 = np.array([0.0, 0.5, 1.0, 1.5, 2.0, 3.0, 4.0, 6.0, -0.0, -0.5, -1.0, -1.5, -2.0, -3.0, -4.0, -6.0])


def pack_weight(w, fmt):
    k, n = w.shape
    w = f64(np.asarray(w, np.float32).astype(ml_dtypes.bfloat16)).reshape(k // 32, 32, n)
    amax = np.abs(w).max(1)
    if fmt == "e4m3":
        byte = np.frexp(amax)[1] - 1 + 127 - 7
    else:
        mant, ex = np.frexp(amax / 6.0)
        byte = np.where(mant > 0.5, ex, ex - 1) + 127
    byte = np.clip(np.where(amax > 0, byte, 1), 1, 254)
    scaled = (w * np.exp2(127.0 - byte)[:, None, :]).reshape(k, n).astype(np.float32)
    by_word = np.ascontiguousarray(scaled.reshape(k // 512, 128, 4, n).transpose(0, 1, 3, 2))
    if fmt == "e4m3":
        words = by_word.astype(ml_dtypes.float8_e4m3fn).view(np.uint8)
    else:
        c = by_word.astype(ml_dtypes.float4_e2m1fn).view(np.uint8) & 0xF
        words = (c[..., 0::2] | (c[..., 1::2] << 4)).reshape(k // 512, 128, 2 * n)
    return np.ascontiguousarray(words), np.ascontiguousarray(byte.astype(np.uint8).reshape(k // 512, 16, n))


def unpack_weight(words, scales, fmt):
    g, _, n = scales.shape
    words = np.ascontiguousarray(words).reshape(g, 128, n, -1)
    if fmt == "e4m3":
        vals = words.view(ml_dtypes.float8_e4m3fn).astype(np.float64)
    else:
        nib = np.empty((g, 128, n, 4), np.uint8)
        nib[..., 0::2] = words & 0xF
        nib[..., 1::2] = words >> 4
        vals = E2M1[nib]
    vals = vals * np.repeat(np.exp2(scales.astype(np.float64) - 127.0), 8, axis=1)[..., None]
    return vals.transpose(0, 1, 3, 2).reshape(g * 512, n)


def gelu(v):
    return 0.5 * v * (1.0 + np.tanh(np.sqrt(2.0 / np.pi) * (v + 0.044715 * v**3)))


def often(T, S):
    return np.random.permutation(T)[(T * np.random.uniform(0, 1, S) ** 4).astype(np.int64)]


def bf(x):
    return np.asarray(x, np.float32).astype(ml_dtypes.bfloat16)


def planes(Y):
    n, m = Y.shape
    b = f64(bf(Y)).reshape(n // 32, 32, m)
    amax = np.abs(b).max(1)
    byte = np.clip(np.where(amax > 0, np.frexp(amax)[1] - 1 + 127 - 7, 1), 1, 254)
    codes = (b * np.exp2(127.0 - byte)[:, None, :]).reshape(n, m).astype(np.float32).astype(ml_dtypes.float8_e4m3fn).view(np.uint8)
    words = codes.reshape(n // 512, 128, 4, m).transpose(0, 1, 3, 2)
    return np.ascontiguousarray(words), np.ascontiguousarray(byte.astype(np.uint8).reshape(n // 512, 16, m))


KP, KV, H, T, T2, S = 1024, 512, 1024, 2048, 1024, 512

def setup_inputs():
    n = np.random.standard_normal
    s = mx_kscale(KP)[:, None]
    s2 = mx_kscale(KV)[:, None]
    u = mx_kscale(H)[:, None]
    unit = np.exp(0.8 * n(H))
    tab_words, tab_scales = pack_weight(n((KP, T)) * s, "e4m3")
    tab2_words, tab2_scales = pack_weight(n((KV, T2)) * s2, "e2m1")
    wp_words, wp_scales = pack_weight(n((KP, H)) * unit / s / np.sqrt(KP), "e2m1")
    w3_words, w3_scales = pack_weight(n((H, H)) / u / np.sqrt(H), "e4m3")
    return {
        "tab_words": tab_words, "tab_scales": tab_scales,
        "tab2_words": tab2_words, "tab2_scales": tab2_scales,
        "offs": striped(often(T, S)),
        "offs2": striped(often(T2, S)),
        "wp_words": wp_words, "wp_scales": wp_scales,
        "wv": (n((KV, H)) * unit / s2 / np.sqrt(KV)).astype(np.float32),
        "gain": (u[:, 0] * np.exp(0.3 * n(H)) / unit).astype(np.float32),
        "w3_words": w3_words, "w3_scales": w3_scales,
    }

def reference(tab_words, tab_scales, tab2_words, tab2_scales, offs, offs2, wp_words, wp_scales, wv, gain, w3_words, w3_scales):
    v = unpack_weight(tab_words, tab_scales, "e4m3")[:, unstriped(offs)]
    v2 = unpack_weight(tab2_words, tab2_scales, "e2m1")[:, unstriped(offs2)]
    wp = unpack_weight(wp_words, wp_scales, "e2m1")
    w3 = unpack_weight(w3_words, w3_scales, "e4m3")
    a = wp.T @ v
    b = mxq(f64(wv), 0, "e4m3").T @ v2
    d = a - b
    z = d * f64(gain)[:, None]
    e = w3.T @ mxq(z, 0, "e4m3")
    gate = 1.0 / (1.0 + np.exp(-e))
    y = b + gate * d
    words, scales = planes(y)
    return y, words, scales

@@ -1,0 +1,295 @@
+from contextlib import ExitStack
+
+import concourse.mybir as mybir
+
+F32 = mybir.dt.float32
+BF16 = mybir.dt.bfloat16
+I32 = mybir.dt.int32
+U32 = mybir.dt.uint32
+U16 = mybir.dt.uint16
+U8 = mybir.dt.uint8
+FP8X4 = mybir.dt.float8_e4m3fn_x4
+FP4X4 = mybir.dt.float4_e2m1fn_x4
+ALU = mybir.AluOpType
+ACT = mybir.ActivationFunctionType
+
+P = 128
+PACK = 4
+KPASS = 512
+H = 1024
+S = 512
+T1 = 2048
+T2 = 1024
+GROUPS = H // KPASS
+HALF = S // 2
+FLOPS = 2 * S * H * (1024 + 512 + 1024)
+
+
+def tile_list_greenhouse_setpoint_gate_kernel(
+    tc, tab_words, tab_scales, tab2_words, tab2_scales, offs, offs2, wp_words, wp_scales,
+    wv, gain, w3_words, w3_scales, out_0, out_1, out_2,
+):
+    nc = tc.nc
+    with ExitStack() as ctx:
+        lists = ctx.enter_context(tc.tile_pool(name="lists", bufs=1))
+        sb = ctx.enter_context(tc.tile_pool(name="sb", bufs=1))
+        held = ctx.enter_context(tc.psum_pool(name="held", bufs=4))
+        ring = ctx.enter_context(tc.psum_pool(name="ring", bufs=4))
+
+        def tile(name, shape, dtype):
+            return sb.tile(shape, dtype, name=name, align_bytes=64)
+
+        idx = lists.tile([P, S // 16], U16, name="idx")
+        idx2 = lists.tile([P, S // 16], U16, name="idx2")
+
+        tab_s = tile("tab_s", [P, T1], U8)
+        tab2_s = tile("tab2_s", [P, T2], U8)
+        w_s_raw = tile("w_s_raw", [P, 2, H], U8)
+        v_s1 = tile("v_s1", [P, S], U8)
+        for plane in (tab_s, w_s_raw, tab2_s, v_s1):
+            nc.vector.memset(plane[:].bitcast(I32), 0)
+
+        tab2_w = tile("tab2_w", [P, T2], U16)
+        wp_raw = tile("wp_raw", [P, 2, H], U16)
+        tab_w = [tile(f"tab_w{a}", [P, T1], I32) for a in range(2)]
+        w3_raw = [tile(f"w3_raw{a}", [P, H], I32) for a in range(2)]
+        wv_raw = [[tile(f"wv_raw{g}{u}", [P, PACK, 256], F32) for u in range(2)] for g in range(GROUPS)]
+        gain_sb = tile("gain_sb", [P, GROUPS, PACK], F32)
+        wv_rows = wv.rearrange("(p i) c -> p i c", i=PACK)
+
+        def load_wv(g, u):
+            c0 = KPASS * g + 256 * u
+            nc.sync.dma_start(out=wv_raw[g][u][:], in_=wv_rows[:, :, c0 : c0 + 256])
+
+        def load_scales(queue, plane, first_row, scales):
+            rows = scales.shape[0] * 4
+            for q in range(4):
+                queue.dma_start(
+                    out=plane[32 * q + first_row : 32 * q + first_row + rows, :].bitcast(I32),
+                    in_=scales.bitcast(I32)[:, 4 * q : 4 * q + 4, :],
+                )
+
+        def load_tab(a):
+            nc.sync.dma_start(out=tab_w[a][:], in_=tab_words[a].rearrange("p t i -> p (t i)").bitcast(I32))
+
+        nc.sync.dma_start(out=tab2_w[:].bitcast(I32), in_=tab2_words[0].bitcast(I32))
+        nc.sync.dma_start(idx2[:], offs2)
+        nc.sync.dma_start(idx[:], offs)
+        load_scales(nc.scalar, tab_s[:], 0, tab_scales)
+        load_scales(nc.gpsimd, w_s_raw[:, 1, :], 4, w3_scales)
+        nc.sync.dma_start(out=wp_raw[:].bitcast(I32), in_=wp_words.bitcast(I32).rearrange("a p c -> p a c"))
+        load_wv(0, 0)
+        load_wv(0, 1)
+        load_scales(nc.sync, tab2_s[:], 0, tab2_scales)
+        load_tab(0)
+        for q in range(4):
+            nc.sync.dma_start(
+                out=w_s_raw[32 * q : 32 * q + 4, :, :].bitcast(I32),
+                in_=wp_scales.bitcast(I32)[:, 4 * q : 4 * q + 4, :].rearrange("a r c -> r a c"),
+            )
+        load_tab(1)
+        nc.sync.dma_start(out=gain_sb[:], in_=gain.rearrange("(g p t) -> p g t", g=GROUPS, t=PACK))
+        load_wv(1, 0)
+        load_wv(1, 1)
+        for a in range(2):
+            nc.sync.dma_start(out=w3_raw[a][:], in_=w3_words[a].rearrange("p c i -> p (c i)").bitcast(I32))
+
+        v2_w = tile("v2_w", [P, S], U16)
+        v2_s = tile("v2_s", [P, S], U8)
+        v_s = tile("v_s", [P, S], U8)
+        v_w = [tile(f"v_w{a}", [P, S], U32) for a in range(2)]
+        nc.vector.tensor_copy(v2_w[:], tab2_w[:].indirect(idx2[:]))
+        nc.vector.tensor_copy(v_s[:], tab_s[:].indirect(idx[:]))
+        nc.gpsimd.dma_start(out=v_s1[0 : P - 4, :].bitcast(I32), in_=v_s[4:P, :].bitcast(I32))
+
+        w_s = [tile(f"w_s{a}", [P, H], U8) for a in range(2)]
+
+        def deal_scales(a):
+            nc.vector.tensor_copy(
+                out=w_s[a][:].rearrange("p (g t c i) -> p g c t i", g=GROUPS, t=PACK, i=16),
+                in_=w_s_raw[:, a, :].rearrange("p (g c i t) -> p g c t i", g=GROUPS, t=PACK, i=16),
+            )
+
+        wp_w = [tile(f"wp_w{g}", [P, 2, KPASS], U16) for g in range(GROUPS)]
+
+        def deal_wp(g):
+            nc.vector.tensor_copy(
+                out=wp_w[g][:].rearrange("p a (t c i) -> p a c t i", t=PACK, i=8),
+                in_=wp_raw[:, :, KPASS * g : KPASS * (g + 1)].rearrange("p a (c i t) -> p a c t i", t=PACK, i=8),
+            )
+
+        nwv_w = [tile(f"nwv_w{g}", [P, KPASS], U32) for g in range(GROUPS)]
+        nwv_s = [tile(f"nwv_s{g}", [P, KPASS], U8) for g in range(GROUPS)]
+
+        def quantise_wv(g):
+            nwv_b = tile(f"nwv_b{g}", [P, PACK, P, PACK], BF16)
+            for u in range(2):
+                nc.scalar.activation(
+                    out=nwv_b[:, :, 64 * u : 64 * (u + 1), :].rearrange("p t m i -> p m i t"),
+                    in_=wv_raw[g][u][:].rearrange("p i (m t) -> p m i t", t=PACK),
+                    func=ACT.Copy,
+                    scale=-1.0,
+                )
+            nc.vector.quantize_mx(
+                out=nwv_w[g][:].bitcast(FP8X4), scales=nwv_s[g][:], in_=nwv_b[:].rearrange("p t m i -> p (t m i)")
+            )
+
+        def plant_passes(bank, g, t, stop):
+            cols = slice(P * t, P * (t + 1))
+            wide = slice(KPASS * g + P * t, KPASS * g + P * (t + 1))
+            for a in range(2):
+                nc.tensor.matmul_mx(
+                    out=bank,
+                    lhsT=wp_w[g][:, a, cols].bitcast(FP4X4),
+                    lhsT_scale=w_s[a][:, wide],
+                    rhs=v_w[a][:].bitcast(FP8X4),
+                    rhs_scale=(v_s, v_s1)[a][:],
+                    start=(a == 0),
+                    stop=(stop and a == 1),
+                )
+
+        def vent_pass(bank, g, t, bays, start):
+            cols = slice(P * t, P * (t + 1))
+            nc.tensor.matmul_mx(
+                out=bank,
+                lhsT=nwv_w[g][:, cols].bitcast(FP8X4),
+                lhsT_scale=nwv_s[g][:, cols],
+                rhs=v2_w[:, bays].bitcast(FP4X4),
+                rhs_scale=v2_s[:, bays],
+                start=start,
+                stop=True,
+            )
+
+        all_bays = slice(0, S)
+        deal_wp(0)
+        deal_wp(1)
+        nc.vector.tensor_copy(v2_s[:], tab2_s[:].indirect(idx2[:]))
+        quantise_wv(0)
+        nb0 = [tile(f"nb0_{h}", [P, PACK, HALF], F32) for h in range(2)]
+        d0 = [tile(f"d0_{h}", [P, PACK, HALF], F32) for h in range(2)]
+        for t in range(PACK):
+            bank = held.tile([P, S], F32, name="held")
+            vent_pass(bank[:], 0, t, all_bays, True)
+            for h in range(2):
+                nc.scalar.copy(out=nb0[h][:, t, :], in_=bank[:, HALF * h : HALF * (h + 1)])
+        nc.vector.tensor_copy(v_w[0][:], tab_w[0][:].bitcast(U32).indirect(idx[:]))
+        deal_scales(0)
+        deal_scales(1)
+        nc.vector.tensor_copy(v_w[1][:], tab_w[1][:].bitcast(U32).indirect(idx[:]))
+
+        a_banks = []
+        for t in range(PACK):
+            bank = ring.tile([P, S], F32, name="ring")
+            plant_passes(bank[:], 0, t, True)
+            a_banks.append(bank)
+        for h in range(2):
+            for t in range(PACK):
+                nc.vector.tensor_tensor(
+                    out=d0[h][:, t, :], in0=a_banks[t][:, HALF * h : HALF * (h + 1)], in1=nb0[h][:, t, :], op=ALU.add
+                )
+
+        z_w = [[tile(f"z_w{g}{h}", [P, HALF], U32) for h in range(2)] for g in range(GROUPS)]
+        z_s = [[tile(f"z_s{g}{h}", [P, HALF], U8) for h in range(2)] for g in range(GROUPS)]
+        z_b = [[tile(f"z_b{g}{h}", [P, HALF, PACK], BF16) for h in range(2)] for g in range(GROUPS)]
+
+        def quantise_z(g, h):
+            nc.vector.quantize_mx(
+                out=z_w[g][h][:].bitcast(FP8X4), scales=z_s[g][h][:], in_=z_b[g][h][:].rearrange("p j t -> p (j t)")
+            )
+
+        d1 = []
+        for t in range(PACK):
+            bank = held.tile([P, S], F32, name="held")
+            plant_passes(bank[:], 1, t, False)
+            d1.append(bank)
+        quantise_wv(1)
+        for t in range(PACK):
+            vent_pass(d1[t][:], 1, t, all_bays, False)
+
+        w3_w = [tile(f"w3_w{a}", [P, H], I32) for a in range(2)]
+        for a in range(2):
+            nc.vector.tensor_copy(
+                out=w3_w[a][:].rearrange("p (g t c i) -> p g c t i", g=GROUPS, t=PACK, i=4),
+                in_=w3_raw[a][:].rearrange("p (g c i t) -> p g c t i", g=GROUPS, t=PACK, i=4),
+            )
+
+        def make_z(g, h):
+            z_rows = tile(f"z_rows{g}{h}", [P, PACK, HALF], BF16)
+            for t in range(PACK):
+                d_rows = d0[h][:, t, :] if g == 0 else d1[t][:, HALF * h : HALF * (h + 1)]
+                nc.scalar.activation(out=z_rows[:, t, :], in_=d_rows, func=ACT.Copy, scale=gain_sb[:, g, t : t + 1])
+            nc.vector.tensor_copy(
+                out=z_b[g][h][:].rearrange("p (c i) t -> p c t i", i=4),
+                in_=z_rows[:].rearrange("p t (c i) -> p c t i", i=4),
+            )
+            quantise_z(g, h)
+
+        for h in range(2):
+            for g in range(GROUPS):
+                make_z(g, h)
+
+        y_s = tile("y_s", [P, GROUPS, S], U8)
+        out_rows = out_0.rearrange("(g p t) j -> g p t j", g=GROUPS, t=PACK)
+        for h in range(2):
+            bays = slice(HALF * h, HALF * (h + 1))
+            th = [tile(f"th{g}{h}", [P, PACK, HALF], F32) for g in range(GROUPS)]
+            for g in (1, 0):
+                for pair in range(2):
+                    bank = ring.tile([P, 2, HALF], F32, name="ring")
+                    for s in range(2):
+                        t = 2 * pair + s
+                        cols = slice(KPASS * g + P * t, KPASS * g + P * (t + 1))
+                        for a in range(2):
+                            nc.tensor.matmul_mx(
+                                out=bank[:, s, :],
+                                lhsT=w3_w[a][:, cols].bitcast(FP8X4),
+                                lhsT_scale=w_s[1][4 + 4 * a : P, cols],
+                                rhs=z_w[a][h][:].bitcast(FP8X4),
+                                rhs_scale=z_s[a][h][:],
+                                start=(a == 0),
+                                stop=(a == 1),
+                            )
+                    nc.scalar.activation(out=th[g][:, 2 * pair : 2 * pair + 2, :], in_=bank[:], func=ACT.Tanh, scale=0.5)
+            nb1 = []
+            for pair in range(2):
+                bank = ring.tile([P, 2, HALF], F32, name="ring")
+                for s in range(2):
+                    vent_pass(bank[:, s, :], 1, 2 * pair + s, bays, True)
+                nb1.append(bank)
+
+            gd = [tile(f"gd{g}{h}", [P, PACK, HALF], F32) for g in range(GROUPS)]
+            y = [tile(f"y{g}{h}", [P, PACK, HALF], F32) for g in range(GROUPS)]
+            for t in range(PACK):
+                nc.vector.scalar_tensor_tensor(
+                    out=gd[1][:, t, :], in0=th[1][:, t, :], scalar=1.0, in1=d1[t][:, bays], op0=ALU.add, op1=ALU.mult
+                )
+            nc.vector.scalar_tensor_tensor(
+                out=gd[0][:], in0=th[0][:], scalar=1.0, in1=d0[h][:], op0=ALU.add, op1=ALU.mult
+            )
+            for pair in range(2):
+                nc.vector.scalar_tensor_tensor(
+                    out=y[1][:, 2 * pair : 2 * pair + 2, :], in0=gd[1][:, 2 * pair : 2 * pair + 2, :], scalar=0.5,
+                    in1=nb1[pair][:], op0=ALU.mult, op1=ALU.subtract,
+                )
+            nc.vector.scalar_tensor_tensor(
+                out=y[0][:], in0=gd[0][:], scalar=0.5, in1=nb0[h][:], op0=ALU.mult, op1=ALU.subtract
+            )
+            for g in (1, 0):
+                nc.sync.dma_start(out=out_rows[g][:, :, bays], in_=y[g][:])
+                y_b = tile(f"y_b{g}{h}", [P, HALF, PACK], BF16)
+                y_w = tile(f"y_w{g}{h}", [P, HALF], U32)
+                nc.scalar.copy(
+                    out=y_b[:].rearrange("p (c i) t -> p c t i", i=4),
+                    in_=y[g][:].rearrange("p t (c i) -> p c t i", i=4),
+                )
+                nc.vector.quantize_mx(
+                    out=y_w[:].bitcast(FP8X4), scales=y_s[:, g, bays], in_=y_b[:].rearrange("p j t -> p (j t)")
+                )
+                nc.sync.dma_start(
+                    out=out_1[g][:, bays, :].rearrange("p j t -> p (j t)").bitcast(I32), in_=y_w[:].bitcast(I32)
+                )
+        for q in range(4):
+            nc.sync.dma_start(
+                out=out_2[:, 4 * q : 4 * q + 4, :].rearrange("g r j -> r g j").bitcast(I32),
+                in_=y_s[32 * q : 32 * q + 4, :, :].bitcast(I32),
+            )

@@ -21,7 +21,7 @@ S = 512
 T1 = 2048
 T2 = 1024
 GROUPS = H // KPASS
-HALF = S // 2
+CHUNKS = ((0, 128), (128, 256), (384, 128))
 FLOPS = 2 * S * H * (1024 + 512 + 1024)
 
 
@@ -50,7 +50,7 @@ def tile_list_greenhouse_setpoint_gate_kernel(
             nc.vector.memset(plane[:].bitcast(I32), 0)
 
         tab2_w = tile("tab2_w", [P, T2], U16)
-        wp_raw = tile("wp_raw", [P, 2, H], U16)
+        wp_raw = [tile(f"wp_raw{g}", [P, 2, KPASS], U16) for g in range(GROUPS)]
         tab_w = [tile(f"tab_w{a}", [P, T1], I32) for a in range(2)]
         w3_raw = [tile(f"w3_raw{a}", [P, H], I32) for a in range(2)]
         wv_raw = [[tile(f"wv_raw{g}{u}", [P, PACK, 256], F32) for u in range(2)] for g in range(GROUPS)]
@@ -69,38 +69,47 @@ def tile_list_greenhouse_setpoint_gate_kernel(
                     in_=scales.bitcast(I32)[:, 4 * q : 4 * q + 4, :],
                 )
 
+        v2_w = tile("v2_w", [P, S], U16)
+        v2_s = tile("v2_s", [P, S], U8)
+        v_s = tile("v_s", [P, S], U8)
+        v_w = [tile(f"v_w{a}", [P, S], U32) for a in range(2)]
+
+        def load_wp(g):
+            pairs = wp_words.bitcast(I32).rearrange("a p c -> p a c")
+            nc.sync.dma_start(out=wp_raw[g][:].bitcast(I32), in_=pairs[:, :, 256 * g : 256 * (g + 1)])
+
         def load_tab(a):
             nc.sync.dma_start(out=tab_w[a][:], in_=tab_words[a].rearrange("p t i -> p (t i)").bitcast(I32))
 
-        nc.sync.dma_start(out=tab2_w[:].bitcast(I32), in_=tab2_words[0].bitcast(I32))
         nc.sync.dma_start(idx2[:], offs2)
+        nc.sync.dma_start(out=tab2_w[:].bitcast(I32), in_=tab2_words[0].bitcast(I32))
         nc.sync.dma_start(idx[:], offs)
-        load_scales(nc.scalar, tab_s[:], 0, tab_scales)
+        for r in range(4):
+            nc.scalar.dma_start(
+                out=tab_s[r:P:16, :].bitcast(I32),
+                in_=tab_scales.bitcast(I32)[:, r:16:4, :].rearrange("a q c -> q a c"),
+            )
         load_scales(nc.gpsimd, w_s_raw[:, 1, :], 4, w3_scales)
-        nc.sync.dma_start(out=wp_raw[:].bitcast(I32), in_=wp_words.bitcast(I32).rearrange("a p c -> p a c"))
+        load_wp(0)
         load_wv(0, 0)
         load_wv(0, 1)
         load_scales(nc.sync, tab2_s[:], 0, tab2_scales)
         load_tab(0)
+        nc.vector.tensor_copy(v2_w[:], tab2_w[:].indirect(idx2[:]))
+        nc.vector.tensor_copy(v_s[:], tab_s[:].indirect(idx[:]))
+        nc.sync.dma_start(out=v_s1[0 : P - 16, :].bitcast(I32), in_=v_s[16:P, :].bitcast(I32))
         for q in range(4):
             nc.sync.dma_start(
                 out=w_s_raw[32 * q : 32 * q + 4, :, :].bitcast(I32),
                 in_=wp_scales.bitcast(I32)[:, 4 * q : 4 * q + 4, :].rearrange("a r c -> r a c"),
             )
         load_tab(1)
+        load_wp(1)
         nc.sync.dma_start(out=gain_sb[:], in_=gain.rearrange("(g p t) -> p g t", g=GROUPS, t=PACK))
         load_wv(1, 0)
         load_wv(1, 1)
         for a in range(2):
             nc.sync.dma_start(out=w3_raw[a][:], in_=w3_words[a].rearrange("p c i -> p (c i)").bitcast(I32))
-
-        v2_w = tile("v2_w", [P, S], U16)
-        v2_s = tile("v2_s", [P, S], U8)
-        v_s = tile("v_s", [P, S], U8)
-        v_w = [tile(f"v_w{a}", [P, S], U32) for a in range(2)]
-        nc.vector.tensor_copy(v2_w[:], tab2_w[:].indirect(idx2[:]))
-        nc.vector.tensor_copy(v_s[:], tab_s[:].indirect(idx[:]))
-        nc.gpsimd.dma_start(out=v_s1[0 : P - 4, :].bitcast(I32), in_=v_s[4:P, :].bitcast(I32))
 
         w_s = [tile(f"w_s{a}", [P, H], U8) for a in range(2)]
 
@@ -115,7 +124,7 @@ def tile_list_greenhouse_setpoint_gate_kernel(
         def deal_wp(g):
             nc.vector.tensor_copy(
                 out=wp_w[g][:].rearrange("p a (t c i) -> p a c t i", t=PACK, i=8),
-                in_=wp_raw[:, :, KPASS * g : KPASS * (g + 1)].rearrange("p a (c i t) -> p a c t i", t=PACK, i=8),
+                in_=wp_raw[g][:].rearrange("p a (c i t) -> p a c t i", t=PACK, i=8),
             )
 
         nwv_w = [tile(f"nwv_w{g}", [P, KPASS], U32) for g in range(GROUPS)]
@@ -134,19 +143,18 @@ def tile_list_greenhouse_setpoint_gate_kernel(
                 out=nwv_w[g][:].bitcast(FP8X4), scales=nwv_s[g][:], in_=nwv_b[:].rearrange("p t m i -> p (t m i)")
             )
 
-        def plant_passes(bank, g, t, stop):
+        def plant_pass(bank, g, t, a, stop):
             cols = slice(P * t, P * (t + 1))
             wide = slice(KPASS * g + P * t, KPASS * g + P * (t + 1))
-            for a in range(2):
-                nc.tensor.matmul_mx(
-                    out=bank,
-                    lhsT=wp_w[g][:, a, cols].bitcast(FP4X4),
-                    lhsT_scale=w_s[a][:, wide],
-                    rhs=v_w[a][:].bitcast(FP8X4),
-                    rhs_scale=(v_s, v_s1)[a][:],
-                    start=(a == 0),
-                    stop=(stop and a == 1),
-                )
+            nc.tensor.matmul_mx(
+                out=bank,
+                lhsT=wp_w[g][:, a, cols].bitcast(FP4X4),
+                lhsT_scale=w_s[a][:, wide],
+                rhs=v_w[a][:].bitcast(FP8X4),
+                rhs_scale=(v_s, v_s1)[a][:],
+                start=(a == 0),
+                stop=stop,
+            )
 
         def vent_pass(bank, g, t, bays, start):
             cols = slice(P * t, P * (t + 1))
@@ -162,49 +170,33 @@ def tile_list_greenhouse_setpoint_gate_kernel(
 
         all_bays = slice(0, S)
         deal_wp(0)
-        deal_wp(1)
         nc.vector.tensor_copy(v2_s[:], tab2_s[:].indirect(idx2[:]))
         quantise_wv(0)
-        nb0 = [tile(f"nb0_{h}", [P, PACK, HALF], F32) for h in range(2)]
-        d0 = [tile(f"d0_{h}", [P, PACK, HALF], F32) for h in range(2)]
+        nb0 = tile("nb0", [P, PACK, S], F32)
+        d0 = tile("d0", [P, PACK, S], F32)
         for t in range(PACK):
             bank = held.tile([P, S], F32, name="held")
             vent_pass(bank[:], 0, t, all_bays, True)
-            for h in range(2):
-                nc.scalar.copy(out=nb0[h][:, t, :], in_=bank[:, HALF * h : HALF * (h + 1)])
+            nc.scalar.copy(out=nb0[:, t, :], in_=bank[:])
         nc.vector.tensor_copy(v_w[0][:], tab_w[0][:].bitcast(U32).indirect(idx[:]))
         deal_scales(0)
+        a_banks = [ring.tile([P, S], F32, name="ring") for t in range(PACK)]
+        d1 = [held.tile([P, S], F32, name="held") for t in range(PACK)]
+        for t in range(PACK):
+            plant_pass(a_banks[t][:], 0, t, 0, False)
         deal_scales(1)
         nc.vector.tensor_copy(v_w[1][:], tab_w[1][:].bitcast(U32).indirect(idx[:]))
-
-        a_banks = []
         for t in range(PACK):
-            bank = ring.tile([P, S], F32, name="ring")
-            plant_passes(bank[:], 0, t, True)
-            a_banks.append(bank)
-        for h in range(2):
+            plant_pass(a_banks[t][:], 0, t, 1, True)
+        deal_wp(1)
+        for a in range(2):
             for t in range(PACK):
-                nc.vector.tensor_tensor(
-                    out=d0[h][:, t, :], in0=a_banks[t][:, HALF * h : HALF * (h + 1)], in1=nb0[h][:, t, :], op=ALU.add
-                )
-
-        z_w = [[tile(f"z_w{g}{h}", [P, HALF], U32) for h in range(2)] for g in range(GROUPS)]
-        z_s = [[tile(f"z_s{g}{h}", [P, HALF], U8) for h in range(2)] for g in range(GROUPS)]
-        z_b = [[tile(f"z_b{g}{h}", [P, HALF, PACK], BF16) for h in range(2)] for g in range(GROUPS)]
-
-        def quantise_z(g, h):
-            nc.vector.quantize_mx(
-                out=z_w[g][h][:].bitcast(FP8X4), scales=z_s[g][h][:], in_=z_b[g][h][:].rearrange("p j t -> p (j t)")
-            )
-
-        d1 = []
-        for t in range(PACK):
-            bank = held.tile([P, S], F32, name="held")
-            plant_passes(bank[:], 1, t, False)
-            d1.append(bank)
+                plant_pass(d1[t][:], 1, t, a, False)
         quantise_wv(1)
         for t in range(PACK):
             vent_pass(d1[t][:], 1, t, all_bays, False)
+        for t in range(PACK):
+            nc.vector.tensor_tensor(out=d0[:, t, :], in0=a_banks[t][:], in1=nb0[:, t, :], op=ALU.add)
 
         w3_w = [tile(f"w3_w{a}", [P, H], I32) for a in range(2)]
         for a in range(2):
@@ -213,71 +205,76 @@ def tile_list_greenhouse_setpoint_gate_kernel(
                 in_=w3_raw[a][:].rearrange("p (g c i t) -> p g c t i", g=GROUPS, t=PACK, i=4),
             )
 
-        def make_z(g, h):
-            z_rows = tile(f"z_rows{g}{h}", [P, PACK, HALF], BF16)
+        def make_z(g, first, width):
+            bays = slice(first, first + width)
+            z_rows = tile(f"z_rows{g}_{first}", [P, PACK, width], BF16)
+            z_b = tile(f"z_b{g}_{first}", [P, width, PACK], BF16)
+            z_w = tile(f"z_w{g}_{first}", [P, width], U32)
+            z_s = tile(f"z_s{g}_{first}", [P, width], U8)
             for t in range(PACK):
-                d_rows = d0[h][:, t, :] if g == 0 else d1[t][:, HALF * h : HALF * (h + 1)]
+                d_rows = d0[:, t, bays] if g == 0 else d1[t][:, bays]
                 nc.scalar.activation(out=z_rows[:, t, :], in_=d_rows, func=ACT.Copy, scale=gain_sb[:, g, t : t + 1])
             nc.vector.tensor_copy(
-                out=z_b[g][h][:].rearrange("p (c i) t -> p c t i", i=4),
+                out=z_b[:].rearrange("p (c i) t -> p c t i", i=4),
                 in_=z_rows[:].rearrange("p t (c i) -> p c t i", i=4),
             )
-            quantise_z(g, h)
+            nc.vector.quantize_mx(out=z_w[:].bitcast(FP8X4), scales=z_s[:], in_=z_b[:].rearrange("p j t -> p (j t)"))
+            return z_w, z_s
 
-        for h in range(2):
-            for g in range(GROUPS):
-                make_z(g, h)
+        z = {}
+        for first, width in CHUNKS:
+            for g in (1, 0):
+                z[g, first] = make_z(g, first, width)
 
         y_s = tile("y_s", [P, GROUPS, S], U8)
         out_rows = out_0.rearrange("(g p t) j -> g p t j", g=GROUPS, t=PACK)
-        for h in range(2):
-            bays = slice(HALF * h, HALF * (h + 1))
-            th = [tile(f"th{g}{h}", [P, PACK, HALF], F32) for g in range(GROUPS)]
+        for first, width in CHUNKS:
+            bays = slice(first, first + width)
+            per_bank = KPASS // width
+            th = [tile(f"th{g}_{first}", [P, PACK, width], F32) for g in range(GROUPS)]
             for g in (1, 0):
-                for pair in range(2):
-                    bank = ring.tile([P, 2, HALF], F32, name="ring")
-                    for s in range(2):
-                        t = 2 * pair + s
-                        cols = slice(KPASS * g + P * t, KPASS * g + P * (t + 1))
+                for t0 in range(0, PACK, per_bank):
+                    bank = ring.tile([P, per_bank, width], F32, name="ring")
+                    for s in range(per_bank):
+                        cols = slice(KPASS * g + P * (t0 + s), KPASS * g + P * (t0 + s + 1))
                         for a in range(2):
                             nc.tensor.matmul_mx(
                                 out=bank[:, s, :],
                                 lhsT=w3_w[a][:, cols].bitcast(FP8X4),
                                 lhsT_scale=w_s[1][4 + 4 * a : P, cols],
-                                rhs=z_w[a][h][:].bitcast(FP8X4),
-                                rhs_scale=z_s[a][h][:],
+                                rhs=z[a, first][0][:].bitcast(FP8X4),
+                                rhs_scale=z[a, first][1][:],
                                 start=(a == 0),
                                 stop=(a == 1),
                             )
-                    nc.scalar.activation(out=th[g][:, 2 * pair : 2 * pair + 2, :], in_=bank[:], func=ACT.Tanh, scale=0.5)
-            nb1 = []
-            for pair in range(2):
-                bank = ring.tile([P, 2, HALF], F32, name="ring")
-                for s in range(2):
-                    vent_pass(bank[:, s, :], 1, 2 * pair + s, bays, True)
-                nb1.append(bank)
+                    nc.scalar.activation(out=th[g][:, t0 : t0 + per_bank, :], in_=bank[:], func=ACT.Tanh, scale=0.5)
+            nb1 = {}
+            for t0 in range(0, PACK, per_bank):
+                nb1[t0] = ring.tile([P, per_bank, width], F32, name="ring")
+                for s in range(per_bank):
+                    vent_pass(nb1[t0][:, s, :], 1, t0 + s, bays, True)
 
-            gd = [tile(f"gd{g}{h}", [P, PACK, HALF], F32) for g in range(GROUPS)]
-            y = [tile(f"y{g}{h}", [P, PACK, HALF], F32) for g in range(GROUPS)]
+            gd = [tile(f"gd{g}_{first}", [P, PACK, width], F32) for g in range(GROUPS)]
+            y = [tile(f"y{g}_{first}", [P, PACK, width], F32) for g in range(GROUPS)]
             for t in range(PACK):
                 nc.vector.scalar_tensor_tensor(
                     out=gd[1][:, t, :], in0=th[1][:, t, :], scalar=1.0, in1=d1[t][:, bays], op0=ALU.add, op1=ALU.mult
                 )
             nc.vector.scalar_tensor_tensor(
-                out=gd[0][:], in0=th[0][:], scalar=1.0, in1=d0[h][:], op0=ALU.add, op1=ALU.mult
+                out=gd[0][:], in0=th[0][:], scalar=1.0, in1=d0[:, :, bays], op0=ALU.add, op1=ALU.mult
             )
-            for pair in range(2):
+            for t0 in range(0, PACK, per_bank):
                 nc.vector.scalar_tensor_tensor(
-                    out=y[1][:, 2 * pair : 2 * pair + 2, :], in0=gd[1][:, 2 * pair : 2 * pair + 2, :], scalar=0.5,
-                    in1=nb1[pair][:], op0=ALU.mult, op1=ALU.subtract,
+                    out=y[1][:, t0 : t0 + per_bank, :], in0=gd[1][:, t0 : t0 + per_bank, :], scalar=0.5,
+                    in1=nb1[t0][:], op0=ALU.mult, op1=ALU.subtract,
                 )
             nc.vector.scalar_tensor_tensor(
-                out=y[0][:], in0=gd[0][:], scalar=0.5, in1=nb0[h][:], op0=ALU.mult, op1=ALU.subtract
+                out=y[0][:], in0=gd[0][:], scalar=0.5, in1=nb0[:, :, bays], op0=ALU.mult, op1=ALU.subtract
             )
             for g in (1, 0):
                 nc.sync.dma_start(out=out_rows[g][:, :, bays], in_=y[g][:])
-                y_b = tile(f"y_b{g}{h}", [P, HALF, PACK], BF16)
-                y_w = tile(f"y_w{g}{h}", [P, HALF], U32)
+                y_b = tile(f"y_b{g}_{first}", [P, width, PACK], BF16)
+                y_w = tile(f"y_w{g}_{first}", [P, width], U32)
                 nc.scalar.copy(
                     out=y_b[:].rearrange("p (c i) t -> p c t i", i=4),
                     in_=y[g][:].rearrange("p t (c i) -> p c t i", i=4),
@@ -289,7 +286,7 @@ def tile_list_greenhouse_setpoint_gate_kernel(
                     out=out_1[g][:, bays, :].rearrange("p j t -> p (j t)").bitcast(I32), in_=y_w[:].bitcast(I32)
                 )
         for q in range(4):
-            nc.sync.dma_start(
+            nc.scalar.dma_start(
                 out=out_2[:, 4 * q : 4 * q + 4, :].rearrange("g r j -> r g j").bitcast(I32),
                 in_=y_s[32 * q : 32 * q + 4, :, :].bitcast(I32),
             )

@@ -36,8 +36,8 @@ def tile_list_greenhouse_setpoint_gate_kernel(
         held = ctx.enter_context(tc.psum_pool(name="held", bufs=4))
         ring = ctx.enter_context(tc.psum_pool(name="ring", bufs=4))
 
-        def tile(name, shape, dtype):
-            return sb.tile(shape, dtype, name=name, align_bytes=64)
+        def tile(name, shape, dtype, tag=None):
+            return sb.tile(shape, dtype, name=name, tag=tag or name, align_bytes=64)
 
         idx = lists.tile([P, S // 16], U16, name="idx")
         idx2 = lists.tile([P, S // 16], U16, name="idx2")
@@ -90,6 +90,7 @@ def tile_list_greenhouse_setpoint_gate_kernel(
                 in_=tab_scales.bitcast(I32)[:, r:16:4, :].rearrange("a q c -> q a c"),
             )
         load_scales(nc.gpsimd, w_s_raw[:, 1, :], 4, w3_scales)
+        nc.gpsimd.dma_start(out=gain_sb[:], in_=gain.rearrange("(g p t) -> p g t", g=GROUPS, t=PACK))
         load_wp(0)
         load_wv(0, 0)
         load_wv(0, 1)
@@ -105,7 +106,6 @@ def tile_list_greenhouse_setpoint_gate_kernel(
             )
         load_tab(1)
         load_wp(1)
-        nc.sync.dma_start(out=gain_sb[:], in_=gain.rearrange("(g p t) -> p g t", g=GROUPS, t=PACK))
         load_wv(1, 0)
         load_wv(1, 1)
         for a in range(2):
@@ -205,9 +205,14 @@ def tile_list_greenhouse_setpoint_gate_kernel(
                 in_=w3_raw[a][:].rearrange("p (g c i t) -> p g c t i", g=GROUPS, t=PACK, i=4),
             )
 
+        z0_rows = tile("z0_rows", [P, PACK * S], BF16, tag="wv_raw11")
+
         def make_z(g, first, width):
             bays = slice(first, first + width)
-            z_rows = tile(f"z_rows{g}_{first}", [P, PACK, width], BF16)
+            if g == 0:
+                z_rows = z0_rows[:, PACK * first : PACK * (first + width)].rearrange("p (t j) -> p t j", t=PACK)
+            else:
+                z_rows = tile(f"z_rows{g}_{first}", [P, PACK, width], BF16)[:]
             z_b = tile(f"z_b{g}_{first}", [P, width, PACK], BF16)
             z_w = tile(f"z_w{g}_{first}", [P, width], U32)
             z_s = tile(f"z_s{g}_{first}", [P, width], U8)
@@ -216,7 +221,7 @@ def tile_list_greenhouse_setpoint_gate_kernel(
                 nc.scalar.activation(out=z_rows[:, t, :], in_=d_rows, func=ACT.Copy, scale=gain_sb[:, g, t : t + 1])
             nc.vector.tensor_copy(
                 out=z_b[:].rearrange("p (c i) t -> p c t i", i=4),
-                in_=z_rows[:].rearrange("p t (c i) -> p c t i", i=4),
+                in_=z_rows.rearrange("p t (c i) -> p c t i", i=4),
             )
             nc.vector.quantize_mx(out=z_w[:].bitcast(FP8X4), scales=z_s[:], in_=z_b[:].rearrange("p j t -> p (j t)"))
             return z_w, z_s
@@ -286,7 +291,7 @@ def tile_list_greenhouse_setpoint_gate_kernel(
                     out=out_1[g][:, bays, :].rearrange("p j t -> p (j t)").bitcast(I32), in_=y_w[:].bitcast(I32)
                 )
         for q in range(4):
-            nc.scalar.dma_start(
+            (nc.scalar, nc.sync, nc.scalar, nc.sync)[q].dma_start(
                 out=out_2[:, 4 * q : 4 * q + 4, :].rearrange("g r j -> r g j").bitcast(I32),
                 in_=y_s[32 * q : 32 * q + 4, :, :].bitcast(I32),
             )

@@ -134,14 +134,18 @@ def tile_list_greenhouse_setpoint_gate_kernel(
             nwv_b = tile(f"nwv_b{g}", [P, PACK, P, PACK], BF16)
             for u in range(2):
                 nc.scalar.activation(
-                    out=nwv_b[:, :, 64 * u : 64 * (u + 1), :].rearrange("p t m i -> p m i t"),
-                    in_=wv_raw[g][u][:].rearrange("p i (m t) -> p m i t", t=PACK),
+                    out=nwv_b[:, :, 64 * u : 64 * (u + 1), :].rearrange("p t m i -> p m t i"),
+                    in_=wv_raw[g][u][:].rearrange("p i (m t) -> p m t i", t=PACK),
                     func=ACT.Copy,
                     scale=-1.0,
                 )
-            nc.vector.quantize_mx(
-                out=nwv_w[g][:].bitcast(FP8X4), scales=nwv_s[g][:], in_=nwv_b[:].rearrange("p t m i -> p (t m i)")
-            )
+            for t0 in (0, 2):
+                cols = slice(P * t0, P * (t0 + 2))
+                nc.vector.quantize_mx(
+                    out=nwv_w[g][:, cols].bitcast(FP8X4),
+                    scales=nwv_s[g][:, cols],
+                    in_=nwv_b[:, t0 : t0 + 2, :, :].rearrange("p t m i -> p (t m i)"),
+                )
 
         def plant_pass(bank, g, t, a, stop):
             cols = slice(P * t, P * (t + 1))
@@ -276,20 +280,20 @@ def tile_list_greenhouse_setpoint_gate_kernel(
             nc.vector.scalar_tensor_tensor(
                 out=y[0][:], in0=gd[0][:], scalar=0.5, in1=nb0[:, :, bays], op0=ALU.mult, op1=ALU.subtract
             )
+            y_w = tile(f"y_w{first}", [P, GROUPS, width], U32)
             for g in (1, 0):
                 nc.sync.dma_start(out=out_rows[g][:, :, bays], in_=y[g][:])
                 y_b = tile(f"y_b{g}_{first}", [P, width, PACK], BF16)
-                y_w = tile(f"y_w{g}_{first}", [P, width], U32)
                 nc.scalar.copy(
                     out=y_b[:].rearrange("p (c i) t -> p c t i", i=4),
                     in_=y[g][:].rearrange("p t (c i) -> p c t i", i=4),
                 )
                 nc.vector.quantize_mx(
-                    out=y_w[:].bitcast(FP8X4), scales=y_s[:, g, bays], in_=y_b[:].rearrange("p j t -> p (j t)")
+                    out=y_w[:, g, :].bitcast(FP8X4), scales=y_s[:, g, bays], in_=y_b[:].rearrange("p j t -> p (j t)")
                 )
-                nc.sync.dma_start(
-                    out=out_1[g][:, bays, :].rearrange("p j t -> p (j t)").bitcast(I32), in_=y_w[:].bitcast(I32)
-                )
+            nc.sync.dma_start(
+                out=out_1[:, :, bays, :].rearrange("g p j t -> p g (j t)").bitcast(I32), in_=y_w[:].bitcast(I32)
+            )
         for q in range(4):
             (nc.scalar, nc.sync, nc.scalar, nc.sync)[q].dma_start(
                 out=out_2[:, 4 * q : 4 * q + 4, :].rearrange("g r j -> r g j").bitcast(I32),

@@ -211,36 +211,40 @@ def tile_list_greenhouse_setpoint_gate_kernel(
 
         z0_rows = tile("z0_rows", [P, PACK * S], BF16, tag="wv_raw11")
 
-        def make_z(g, first, width):
+        z = {}
+
+        z_rows = {}
+
+        def scale_z(g, first, width):
             bays = slice(first, first + width)
             if g == 0:
-                z_rows = z0_rows[:, PACK * first : PACK * (first + width)].rearrange("p (t j) -> p t j", t=PACK)
+                rows = z0_rows[:, PACK * first : PACK * (first + width)].rearrange("p (t j) -> p t j", t=PACK)
             else:
-                z_rows = tile(f"z_rows{g}_{first}", [P, PACK, width], BF16)[:]
-            z_b = tile(f"z_b{g}_{first}", [P, width, PACK], BF16)
-            z_w = tile(f"z_w{g}_{first}", [P, width], U32)
-            z_s = tile(f"z_s{g}_{first}", [P, width], U8)
+                rows = tile(f"z_rows{g}_{first}", [P, PACK, width], BF16)[:]
             for t in range(PACK):
                 d_rows = d0[:, t, bays] if g == 0 else d1[t][:, bays]
-                nc.scalar.activation(out=z_rows[:, t, :], in_=d_rows, func=ACT.Copy, scale=gain_sb[:, g, t : t + 1])
-            nc.vector.tensor_copy(
+                nc.scalar.activation(out=rows[:, t, :], in_=d_rows, func=ACT.Copy, scale=gain_sb[:, g, t : t + 1])
+            z_rows[g, first] = rows
+
+        def quantise_z(g, first, width, weave, tag=None):
+            z_b = tile(f"z_b{g}_{first}", [P, width, PACK], BF16, tag=tag)
+            z_w = tile(f"z_w{g}_{first}", [P, width], U32)
+            z_s = tile(f"z_s{g}_{first}", [P, width], U8)
+            weave(
                 out=z_b[:].rearrange("p (c i) t -> p c t i", i=4),
-                in_=z_rows.rearrange("p t (c i) -> p c t i", i=4),
+                in_=z_rows[g, first].rearrange("p t (c i) -> p c t i", i=4),
             )
             nc.vector.quantize_mx(out=z_w[:].bitcast(FP8X4), scales=z_s[:], in_=z_b[:].rearrange("p j t -> p (j t)"))
-            return z_w, z_s
-
-        z = {}
-        for first, width in CHUNKS:
-            for g in (1, 0):
-                z[g, first] = make_z(g, first, width)
+            z[g, first] = (z_w, z_s)
 
         y_s = tile("y_s", [P, GROUPS, S], U8)
         out_rows = out_0.rearrange("(g p t) j -> g p t j", g=GROUPS, t=PACK)
-        for first, width in CHUNKS:
-            bays = slice(first, first + width)
+        gates, results = {}, {}
+
+        def gate(first, width):
             per_bank = KPASS // width
             th = [tile(f"th{g}_{first}", [P, PACK, width], F32) for g in range(GROUPS)]
+            gates[first] = th
             for g in (1, 0):
                 for t0 in range(0, PACK, per_bank):
                     bank = ring.tile([P, per_bank, width], F32, name="ring")
@@ -257,6 +261,11 @@ def tile_list_greenhouse_setpoint_gate_kernel(
                                 stop=(a == 1),
                             )
                     nc.scalar.activation(out=th[g][:, t0 : t0 + per_bank, :], in_=bank[:], func=ACT.Tanh, scale=0.5)
+
+        def mix(first, width):
+            bays = slice(first, first + width)
+            per_bank = KPASS // width
+            th = gates[first]
             nb1 = {}
             for t0 in range(0, PACK, per_bank):
                 nb1[t0] = ring.tile([P, per_bank, width], F32, name="ring")
@@ -280,11 +289,16 @@ def tile_list_greenhouse_setpoint_gate_kernel(
             nc.vector.scalar_tensor_tensor(
                 out=y[0][:], in0=gd[0][:], scalar=0.5, in1=nb0[:, :, bays], op0=ALU.mult, op1=ALU.subtract
             )
+            results[first] = y
+
+        def hand_out(first, width):
+            bays = slice(first, first + width)
+            y = results[first]
             y_w = tile(f"y_w{first}", [P, GROUPS, width], U32)
             for g in (1, 0):
                 nc.sync.dma_start(out=out_rows[g][:, :, bays], in_=y[g][:])
                 y_b = tile(f"y_b{g}_{first}", [P, width, PACK], BF16)
-                nc.scalar.copy(
+                (nc.vector.tensor_copy if g == 0 and first + width == S else nc.scalar.copy)(
                     out=y_b[:].rearrange("p (c i) t -> p c t i", i=4),
                     in_=y[g][:].rearrange("p t (c i) -> p c t i", i=4),
                 )
@@ -294,6 +308,25 @@ def tile_list_greenhouse_setpoint_gate_kernel(
             nc.sync.dma_start(
                 out=out_1[:, :, bays, :].rearrange("g p j t -> p g (j t)").bitcast(I32), in_=y_w[:].bitcast(I32)
             )
+
+        head, middle, last = CHUNKS
+        for piece in (head, middle):
+            for g in (1, 0):
+                scale_z(g, *piece)
+                quantise_z(g, *piece, nc.vector.tensor_copy)
+        for g in (1, 0):
+            scale_z(g, *last)
+        gate(*head)
+        mix(*head)
+        for g in (1, 0):
+            quantise_z(g, *last, nc.scalar.copy, f"th{g}_0")
+        gate(*middle)
+        hand_out(*head)
+        mix(*middle)
+        gate(*last)
+        hand_out(*middle)
+        mix(*last)
+        hand_out(*last)
         for q in range(4):
             (nc.scalar, nc.sync, nc.scalar, nc.sync)[q].dma_start(
                 out=out_2[:, 4 * q : 4 * q + 4, :].rearrange("g r j -> r g j").bitcast(I32),

@@ -98,13 +98,13 @@ def tile_list_greenhouse_setpoint_gate_kernel(
         load_tab(0)
         nc.vector.tensor_copy(v2_w[:], tab2_w[:].indirect(idx2[:]))
         nc.vector.tensor_copy(v_s[:], tab_s[:].indirect(idx[:]))
-        nc.sync.dma_start(out=v_s1[0 : P - 16, :].bitcast(I32), in_=v_s[16:P, :].bitcast(I32))
         for q in range(4):
             nc.sync.dma_start(
                 out=w_s_raw[32 * q : 32 * q + 4, :, :].bitcast(I32),
                 in_=wp_scales.bitcast(I32)[:, 4 * q : 4 * q + 4, :].rearrange("a r c -> r a c"),
             )
         load_tab(1)
+        nc.sync.dma_start(out=v_s1[0 : P - 16, :].bitcast(I32), in_=v_s[16:P, :].bitcast(I32))
         load_wp(1)
         load_wv(1, 0)
         load_wv(1, 1)

@@ -114,7 +114,7 @@ def tile_list_greenhouse_setpoint_gate_kernel(
         w_s = [tile(f"w_s{a}", [P, H], U8) for a in range(2)]
 
         def deal_scales(a):
-            nc.vector.tensor_copy(
+            (nc.vector, nc.gpsimd)[a].tensor_copy(
                 out=w_s[a][:].rearrange("p (g t c i) -> p g c t i", g=GROUPS, t=PACK, i=16),
                 in_=w_s_raw[:, a, :].rearrange("p (g c i t) -> p g c t i", g=GROUPS, t=PACK, i=16),
             )

@@ -286,9 +286,13 @@ def tile_list_greenhouse_setpoint_gate_kernel(
                     out=y[1][:, t0 : t0 + per_bank, :], in0=gd[1][:, t0 : t0 + per_bank, :], scalar=0.5,
                     in1=nb1[t0][:], op0=ALU.mult, op1=ALU.subtract,
                 )
-            nc.vector.scalar_tensor_tensor(
-                out=y[0][:], in0=gd[0][:], scalar=0.5, in1=nb0[:, :, bays], op0=ALU.mult, op1=ALU.subtract
-            )
+            halves = 2 if first + width == S else 1
+            for h in range(halves):
+                part = slice(width // halves * h, width // halves * (h + 1))
+                nc.vector.scalar_tensor_tensor(
+                    out=y[0][:, :, part], in0=gd[0][:, :, part], scalar=0.5,
+                    in1=nb0[:, :, first + part.start : first + part.stop], op0=ALU.mult, op1=ALU.subtract,
+                )
             results[first] = y
 
         def hand_out(first, width):
@@ -298,10 +302,14 @@ def tile_list_greenhouse_setpoint_gate_kernel(
             for g in (1, 0):
                 nc.sync.dma_start(out=out_rows[g][:, :, bays], in_=y[g][:])
                 y_b = tile(f"y_b{g}_{first}", [P, width, PACK], BF16)
-                (nc.vector.tensor_copy if g == 0 and first + width == S else nc.scalar.copy)(
-                    out=y_b[:].rearrange("p (c i) t -> p c t i", i=4),
-                    in_=y[g][:].rearrange("p t (c i) -> p c t i", i=4),
-                )
+                very_last = g == 0 and first + width == S
+                halves = 2 if very_last else 1
+                for h in range(halves):
+                    part = slice(width // halves * h, width // halves * (h + 1))
+                    (nc.vector.tensor_copy if very_last else nc.scalar.copy)(
+                        out=y_b[:, part, :].rearrange("p (c i) t -> p c t i", i=4),
+                        in_=y[g][:, :, part].rearrange("p t (c i) -> p c t i", i=4),
+                    )
                 nc.vector.quantize_mx(
                     out=y_w[:, g, :].bitcast(FP8X4), scales=y_s[:, g, bays], in_=y_b[:].rearrange("p j t -> p (j t)")
                 )

@@ -94,14 +94,15 @@ def tile_list_greenhouse_setpoint_gate_kernel(
         load_wp(0)
         load_wv(0, 0)
         load_wv(0, 1)
-        load_scales(nc.sync, tab2_s[:], 0, tab2_scales)
+        for r in range(4):
+            nc.sync.dma_start(out=tab2_s[r:P:32, :].bitcast(I32), in_=tab2_scales.bitcast(I32)[0, r:16:4, :])
         load_tab(0)
         nc.vector.tensor_copy(v2_w[:], tab2_w[:].indirect(idx2[:]))
         nc.vector.tensor_copy(v_s[:], tab_s[:].indirect(idx[:]))
-        for q in range(4):
+        for r in range(4):
             nc.sync.dma_start(
-                out=w_s_raw[32 * q : 32 * q + 4, :, :].bitcast(I32),
-                in_=wp_scales.bitcast(I32)[:, 4 * q : 4 * q + 4, :].rearrange("a r c -> r a c"),
+                out=w_s_raw[r:P:32, :, :].bitcast(I32),
+                in_=wp_scales.bitcast(I32)[:, r:16:4, :].rearrange("a q c -> q a c"),
             )
         load_tab(1)
         nc.sync.dma_start(out=v_s1[0 : P - 16, :].bitcast(I32), in_=v_s[16:P, :].bitcast(I32))

@@ -91,9 +91,9 @@ def tile_list_greenhouse_setpoint_gate_kernel(
             )
         load_scales(nc.gpsimd, w_s_raw[:, 1, :], 4, w3_scales)
         nc.gpsimd.dma_start(out=gain_sb[:], in_=gain.rearrange("(g p t) -> p g t", g=GROUPS, t=PACK))
-        load_wp(0)
         load_wv(0, 0)
         load_wv(0, 1)
+        load_wp(0)
         for r in range(4):
             nc.sync.dma_start(out=tab2_s[r:P:32, :].bitcast(I32), in_=tab2_scales.bitcast(I32)[0, r:16:4, :])
         load_tab(0)

@@ -124,8 +124,8 @@ def tile_list_greenhouse_setpoint_gate_kernel(
 
         def deal_wp(g):
             nc.vector.tensor_copy(
-                out=wp_w[g][:].rearrange("p a (t c i) -> p a c t i", t=PACK, i=8),
-                in_=wp_raw[g][:].rearrange("p a (c i t) -> p a c t i", t=PACK, i=8),
+                out=wp_w[g][:].rearrange("p a (u e m) -> p a u m e", u=2, e=2),
+                in_=wp_raw[g][:].rearrange("p a (m u e) -> p a u m e", u=2, e=2),
             )
 
         nwv_w = [tile(f"nwv_w{g}", [P, KPASS], U32) for g in range(GROUPS)]
@@ -135,8 +135,8 @@ def tile_list_greenhouse_setpoint_gate_kernel(
             nwv_b = tile(f"nwv_b{g}", [P, PACK, P, PACK], BF16)
             for u in range(2):
                 nc.scalar.activation(
-                    out=nwv_b[:, :, 64 * u : 64 * (u + 1), :].rearrange("p t m i -> p m t i"),
-                    in_=wv_raw[g][u][:].rearrange("p i (m t) -> p m t i", t=PACK),
+                    out=nwv_b[:, :, 64 * u : 64 * (u + 1), :].rearrange("p t m i -> p m i t"),
+                    in_=wv_raw[g][u][:].rearrange("p i (m t) -> p m i t", t=PACK),
                     func=ACT.Copy,
                     scale=-1.0,
                 )
@@ -206,8 +206,8 @@ def tile_list_greenhouse_setpoint_gate_kernel(
         w3_w = [tile(f"w3_w{a}", [P, H], I32) for a in range(2)]
         for a in range(2):
             nc.vector.tensor_copy(
-                out=w3_w[a][:].rearrange("p (g t c i) -> p g c t i", g=GROUPS, t=PACK, i=4),
-                in_=w3_raw[a][:].rearrange("p (g c i t) -> p g c t i", g=GROUPS, t=PACK, i=4),
+                out=w3_w[a][:].rearrange("p (g u e m) -> p g u m e", g=GROUPS, u=2, e=2),
+                in_=w3_raw[a][:].rearrange("p (g m u e) -> p g u m e", g=GROUPS, u=2, e=2),
             )
 
         z0_rows = tile("z0_rows", [P, PACK * S], BF16, tag="wv_raw11")
@@ -308,8 +308,8 @@ def tile_list_greenhouse_setpoint_gate_kernel(
                 for h in range(halves):
                     part = slice(width // halves * h, width // halves * (h + 1))
                     (nc.vector.tensor_copy if very_last else nc.scalar.copy)(
-                        out=y_b[:, part, :].rearrange("p (c i) t -> p c t i", i=4),
-                        in_=y[g][:, :, part].rearrange("p t (c i) -> p c t i", i=4),
+                        out=y_b[:, part, :].rearrange("p (c i) t -> p c t i", i=2),
+                        in_=y[g][:, :, part].rearrange("p t (c i) -> p c t i", i=2),
                     )
                 nc.vector.quantize_mx(
                     out=y_w[:, g, :].bitcast(FP8X4), scales=y_s[:, g, bays], in_=y_b[:].rearrange("p j t -> p (j t)")

@@ -178,7 +178,7 @@ def tile_list_greenhouse_setpoint_gate_kernel(
         nc.vector.tensor_copy(v2_s[:], tab2_s[:].indirect(idx2[:]))
         quantise_wv(0)
         nb0 = tile("nb0", [P, PACK, S], F32)
-        d0 = tile("d0", [P, PACK, S], F32)
+        d0 = tile("d0", [P, PACK, S], F32, tag="wp_raw1")
         for t in range(PACK):
             bank = held.tile([P, S], F32, name="held")
             vent_pass(bank[:], 0, t, all_bays, True)

@@ -33,11 +33,13 @@ def tile_list_greenhouse_setpoint_gate_kernel(
     with ExitStack() as ctx:
         lists = ctx.enter_context(tc.tile_pool(name="lists", bufs=1))
         sb = ctx.enter_context(tc.tile_pool(name="sb", bufs=1))
-        held = ctx.enter_context(tc.psum_pool(name="held", bufs=4))
-        ring = ctx.enter_context(tc.psum_pool(name="ring", bufs=4))
+        banks = ctx.enter_context(tc.psum_pool(name="banks", bufs=1))
 
         def tile(name, shape, dtype, tag=None):
             return sb.tile(shape, dtype, name=name, tag=tag or name, align_bytes=64)
+
+        def bank_tile(number, shape):
+            return banks.tile(shape, F32, name=f"bank{number}")
 
         idx = lists.tile([P, S // 16], U16, name="idx")
         idx2 = lists.tile([P, S // 16], U16, name="idx2")
@@ -148,20 +150,20 @@ def tile_list_greenhouse_setpoint_gate_kernel(
                     in_=nwv_b[:, t0 : t0 + 2, :, :].rearrange("p t m i -> p (t m i)"),
                 )
 
-        def plant_pass(bank, g, t, a, stop):
+        def plant_pass(bank, g, t, a, bays, start, stop):
             cols = slice(P * t, P * (t + 1))
             wide = slice(KPASS * g + P * t, KPASS * g + P * (t + 1))
             nc.tensor.matmul_mx(
                 out=bank,
                 lhsT=wp_w[g][:, a, cols].bitcast(FP4X4),
                 lhsT_scale=w_s[a][:, wide],
-                rhs=v_w[a][:].bitcast(FP8X4),
-                rhs_scale=(v_s, v_s1)[a][:],
-                start=(a == 0),
+                rhs=v_w[a][:, bays].bitcast(FP8X4),
+                rhs_scale=(v_s, v_s1)[a][:, bays],
+                start=start,
                 stop=stop,
             )
 
-        def vent_pass(bank, g, t, bays, start):
+        def vent_pass(bank, g, t, bays, start, stop=True):
             cols = slice(P * t, P * (t + 1))
             nc.tensor.matmul_mx(
                 out=bank,
@@ -170,7 +172,7 @@ def tile_list_greenhouse_setpoint_gate_kernel(
                 rhs=v2_w[:, bays].bitcast(FP4X4),
                 rhs_scale=v2_s[:, bays],
                 start=start,
-                stop=True,
+                stop=stop,
             )
 
         all_bays = slice(0, S)
@@ -180,26 +182,40 @@ def tile_list_greenhouse_setpoint_gate_kernel(
         nb0 = tile("nb0", [P, PACK, S], F32)
         d0 = tile("d0", [P, PACK, S], F32, tag="wp_raw1")
         for t in range(PACK):
-            bank = held.tile([P, S], F32, name="held")
+            bank = bank_tile(t, [P, S])
             vent_pass(bank[:], 0, t, all_bays, True)
             nc.scalar.copy(out=nb0[:, t, :], in_=bank[:])
         nc.vector.tensor_copy(v_w[0][:], tab_w[0][:].bitcast(U32).indirect(idx[:]))
         deal_scales(0)
-        a_banks = [ring.tile([P, S], F32, name="ring") for t in range(PACK)]
-        d1 = [held.tile([P, S], F32, name="held") for t in range(PACK)]
+        a_banks = [bank_tile(PACK + t, [P, S]) for t in range(PACK)]
         for t in range(PACK):
-            plant_pass(a_banks[t][:], 0, t, 0, False)
+            plant_pass(a_banks[t][:], 0, t, 0, all_bays, True, False)
         deal_scales(1)
         nc.vector.tensor_copy(v_w[1][:], tab_w[1][:].bitcast(U32).indirect(idx[:]))
         for t in range(PACK):
-            plant_pass(a_banks[t][:], 0, t, 1, True)
+            plant_pass(a_banks[t][:], 0, t, 1, all_bays, False, True)
         deal_wp(1)
-        for a in range(2):
-            for t in range(PACK):
-                plant_pass(d1[t][:], 1, t, a, False)
         quantise_wv(1)
-        for t in range(PACK):
-            vent_pass(d1[t][:], 1, t, all_bays, False)
+        d1 = {}
+
+        def difference(first, width):
+            bays = slice(first, first + width)
+            per_bank = KPASS // width
+            for t0 in range(0, PACK, per_bank):
+                bank = bank_tile(first // P + t0 // per_bank, [P, per_bank, width])
+                d1[first, t0] = bank
+                products = ("vent", 1, 0) if first + width == S else (1, 0, "vent")
+                for k, a in enumerate(products):
+                    for s in range(per_bank):
+                        start, stop = (k, s) == (0, 0), (k, s) == (2, per_bank - 1)
+                        if a == "vent":
+                            vent_pass(bank[:, s, :], 1, t0 + s, bays, start, stop)
+                        else:
+                            plant_pass(bank[:, s, :], 1, t0 + s, a, bays, start, stop)
+
+        head, middle, last = CHUNKS
+        difference(*head)
+        difference(*middle)
         for t in range(PACK):
             nc.vector.tensor_tensor(out=d0[:, t, :], in0=a_banks[t][:], in1=nb0[:, t, :], op=ALU.add)
 
@@ -223,7 +239,8 @@ def tile_list_greenhouse_setpoint_gate_kernel(
             else:
                 rows = tile(f"z_rows{g}_{first}", [P, PACK, width], BF16)[:]
             for t in range(PACK):
-                d_rows = d0[:, t, bays] if g == 0 else d1[t][:, bays]
+                per_bank = KPASS // width
+                d_rows = d0[:, t, bays] if g == 0 else d1[first, t - t % per_bank][:, t % per_bank, :]
                 nc.scalar.activation(out=rows[:, t, :], in_=d_rows, func=ACT.Copy, scale=gain_sb[:, g, t : t + 1])
             z_rows[g, first] = rows
 
@@ -231,10 +248,18 @@ def tile_list_greenhouse_setpoint_gate_kernel(
             z_b = tile(f"z_b{g}_{first}", [P, width, PACK], BF16, tag=tag)
             z_w = tile(f"z_w{g}_{first}", [P, width], U32)
             z_s = tile(f"z_s{g}_{first}", [P, width], U8)
-            weave(
-                out=z_b[:].rearrange("p (c i) t -> p c t i", i=4),
-                in_=z_rows[g, first].rearrange("p t (c i) -> p c t i", i=4),
-            )
+            if weave is None:
+                nc.vector.tensor_tensor(
+                    out=z_b[:].rearrange("p (c i) t -> p c t i", i=2),
+                    in0=d1[first, 0][:].rearrange("p t (c i) -> p c t i", i=2),
+                    in1=gain_sb[:, 1, :].unsqueeze(1).unsqueeze(3).to_broadcast([P, width // 2, PACK, 2]),
+                    op=ALU.mult,
+                )
+            else:
+                weave(
+                    out=z_b[:].rearrange("p (c i) t -> p c t i", i=4),
+                    in_=z_rows[g, first].rearrange("p t (c i) -> p c t i", i=4),
+                )
             nc.vector.quantize_mx(out=z_w[:].bitcast(FP8X4), scales=z_s[:], in_=z_b[:].rearrange("p j t -> p (j t)"))
             z[g, first] = (z_w, z_s)
 
@@ -246,20 +271,21 @@ def tile_list_greenhouse_setpoint_gate_kernel(
             per_bank = KPASS // width
             th = [tile(f"th{g}_{first}", [P, PACK, width], F32) for g in range(GROUPS)]
             gates[first] = th
+            numbers = list({0: (4, 5), 128: (7, 4, 5, 0), 384: (4, 5)}[first])
             for g in (1, 0):
                 for t0 in range(0, PACK, per_bank):
-                    bank = ring.tile([P, per_bank, width], F32, name="ring")
-                    for s in range(per_bank):
-                        cols = slice(KPASS * g + P * (t0 + s), KPASS * g + P * (t0 + s + 1))
-                        for a in range(2):
+                    bank = bank_tile(numbers.pop(0), [P, per_bank, width])
+                    for a in range(2):
+                        for s in range(per_bank):
+                            cols = slice(KPASS * g + P * (t0 + s), KPASS * g + P * (t0 + s + 1))
                             nc.tensor.matmul_mx(
                                 out=bank[:, s, :],
                                 lhsT=w3_w[a][:, cols].bitcast(FP8X4),
                                 lhsT_scale=w_s[1][4 + 4 * a : P, cols],
                                 rhs=z[a, first][0][:].bitcast(FP8X4),
                                 rhs_scale=z[a, first][1][:],
-                                start=(a == 0),
-                                stop=(a == 1),
+                                start=(a, s) == (0, 0),
+                                stop=(a, s) == (1, per_bank - 1),
                             )
                     nc.scalar.activation(out=th[g][:, t0 : t0 + per_bank, :], in_=bank[:], func=ACT.Tanh, scale=0.5)
 
@@ -269,15 +295,16 @@ def tile_list_greenhouse_setpoint_gate_kernel(
             th = gates[first]
             nb1 = {}
             for t0 in range(0, PACK, per_bank):
-                nb1[t0] = ring.tile([P, per_bank, width], F32, name="ring")
+                nb1[t0] = bank_tile({0: (6,), 128: (6, 7), 384: (1,)}[first][t0 // per_bank], [P, per_bank, width])
                 for s in range(per_bank):
                     vent_pass(nb1[t0][:, s, :], 1, t0 + s, bays, True)
 
             gd = [tile(f"gd{g}_{first}", [P, PACK, width], F32) for g in range(GROUPS)]
             y = [tile(f"y{g}_{first}", [P, PACK, width], F32) for g in range(GROUPS)]
-            for t in range(PACK):
+            for t0 in range(0, PACK, per_bank):
                 nc.vector.scalar_tensor_tensor(
-                    out=gd[1][:, t, :], in0=th[1][:, t, :], scalar=1.0, in1=d1[t][:, bays], op0=ALU.add, op1=ALU.mult
+                    out=gd[1][:, t0 : t0 + per_bank, :], in0=th[1][:, t0 : t0 + per_bank, :], scalar=1.0,
+                    in1=d1[first, t0][:], op0=ALU.add, op1=ALU.mult,
                 )
             nc.vector.scalar_tensor_tensor(
                 out=gd[0][:], in0=th[0][:], scalar=1.0, in1=d0[:, :, bays], op0=ALU.add, op1=ALU.mult
@@ -307,7 +334,7 @@ def tile_list_greenhouse_setpoint_gate_kernel(
                 halves = 2 if very_last else 1
                 for h in range(halves):
                     part = slice(width // halves * h, width // halves * (h + 1))
-                    (nc.vector.tensor_copy if very_last else nc.scalar.copy)(
+                    nc.scalar.copy(
                         out=y_b[:, part, :].rearrange("p (c i) t -> p c t i", i=2),
                         in_=y[g][:, :, part].rearrange("p t (c i) -> p c t i", i=2),
                     )
@@ -318,17 +345,19 @@ def tile_list_greenhouse_setpoint_gate_kernel(
                 out=out_1[:, :, bays, :].rearrange("g p j t -> p g (j t)").bitcast(I32), in_=y_w[:].bitcast(I32)
             )
 
-        head, middle, last = CHUNKS
-        for piece in (head, middle):
-            for g in (1, 0):
-                scale_z(g, *piece)
-                quantise_z(g, *piece, nc.vector.tensor_copy)
+        quantise_z(1, *head, None)
+        scale_z(0, *head)
+        quantise_z(0, *head, nc.vector.tensor_copy)
+        for g in (1, 0):
+            scale_z(g, *middle)
+            quantise_z(g, *middle, nc.vector.tensor_copy)
+        gate(*head)
+        difference(*last)
         for g in (1, 0):
             scale_z(g, *last)
-        gate(*head)
         mix(*head)
         for g in (1, 0):
-            quantise_z(g, *last, nc.scalar.copy, f"th{g}_0")
+            quantise_z(g, *last, nc.scalar.copy, f"z_w{g}_0")
         gate(*middle)
         hand_out(*head)
         mix(*middle)

@@ -323,23 +323,31 @@ def tile_list_greenhouse_setpoint_gate_kernel(
                 )
             results[first] = y
 
-        def hand_out(first, width):
+        rounded_y = {}
+
+        def round_y(first, width):
             bays = slice(first, first + width)
             y = results[first]
-            y_w = tile(f"y_w{first}", [P, GROUPS, width], U32)
             for g in (1, 0):
                 nc.sync.dma_start(out=out_rows[g][:, :, bays], in_=y[g][:])
                 y_b = tile(f"y_b{g}_{first}", [P, width, PACK], BF16)
-                very_last = g == 0 and first + width == S
-                halves = 2 if very_last else 1
+                halves = 2 if g == 0 and first + width == S else 1
                 for h in range(halves):
                     part = slice(width // halves * h, width // halves * (h + 1))
                     nc.scalar.copy(
                         out=y_b[:, part, :].rearrange("p (c i) t -> p c t i", i=2),
                         in_=y[g][:, :, part].rearrange("p t (c i) -> p c t i", i=2),
                     )
+                rounded_y[g, first] = y_b
+
+        def quantise_y(first, width):
+            bays = slice(first, first + width)
+            y_w = tile(f"y_w{first}", [P, GROUPS, width], U32)
+            for g in (1, 0):
                 nc.vector.quantize_mx(
-                    out=y_w[:, g, :].bitcast(FP8X4), scales=y_s[:, g, bays], in_=y_b[:].rearrange("p j t -> p (j t)")
+                    out=y_w[:, g, :].bitcast(FP8X4),
+                    scales=y_s[:, g, bays],
+                    in_=rounded_y[g, first][:].rearrange("p j t -> p (j t)"),
                 )
             nc.sync.dma_start(
                 out=out_1[:, :, bays, :].rearrange("g p j t -> p g (j t)").bitcast(I32), in_=y_w[:].bitcast(I32)
@@ -359,12 +367,15 @@ def tile_list_greenhouse_setpoint_gate_kernel(
         for g in (1, 0):
             quantise_z(g, *last, nc.scalar.copy, f"z_w{g}_0")
         gate(*middle)
-        hand_out(*head)
+        round_y(*head)
+        quantise_y(*head)
         mix(*middle)
         gate(*last)
-        hand_out(*middle)
+        round_y(*middle)
         mix(*last)
-        hand_out(*last)
+        round_y(*last)
+        quantise_y(*middle)
+        quantise_y(*last)
         for q in range(4):
             (nc.scalar, nc.sync, nc.scalar, nc.sync)[q].dma_start(
                 out=out_2[:, 4 * q : 4 * q + 4, :].rearrange("g r j -> r g j").bitcast(I32),

from contextlib import ExitStack

import concourse.mybir as mybir

F32 = mybir.dt.float32
BF16 = mybir.dt.bfloat16
I32 = mybir.dt.int32
U32 = mybir.dt.uint32
U16 = mybir.dt.uint16
U8 = mybir.dt.uint8
FP8X4 = mybir.dt.float8_e4m3fn_x4
FP4X4 = mybir.dt.float4_e2m1fn_x4
ALU = mybir.AluOpType
ACT = mybir.ActivationFunctionType

P = 128
PACK = 4
KPASS = 512
H = 1024
S = 512
T1 = 2048
T2 = 1024
GROUPS = H // KPASS
CHUNKS = ((0, 128), (128, 256), (384, 128))
FLOPS = 2 * S * H * (1024 + 512 + 1024)


def tile_list_greenhouse_setpoint_gate_kernel(
    tc, tab_words, tab_scales, tab2_words, tab2_scales, offs, offs2, wp_words, wp_scales,
    wv, gain, w3_words, w3_scales, out_0, out_1, out_2,
):
    nc = tc.nc
    with ExitStack() as ctx:
        lists = ctx.enter_context(tc.tile_pool(name="lists", bufs=1))
        sb = ctx.enter_context(tc.tile_pool(name="sb", bufs=1))
        banks = ctx.enter_context(tc.psum_pool(name="banks", bufs=1))

        def tile(name, shape, dtype, tag=None):
            return sb.tile(shape, dtype, name=name, tag=tag or name, align_bytes=64)

        def bank_tile(number, shape):
            return banks.tile(shape, F32, name=f"bank{number}")

        idx = lists.tile([P, S // 16], U16, name="idx")
        idx2 = lists.tile([P, S // 16], U16, name="idx2")

        tab_s = tile("tab_s", [P, T1], U8)
        tab2_s = tile("tab2_s", [P, T2], U8)
        w_s_raw = tile("w_s_raw", [P, 2, H], U8)
        v_s1 = tile("v_s1", [P, S], U8)
        for plane in (tab_s, w_s_raw, tab2_s, v_s1):
            nc.vector.memset(plane[:].bitcast(I32), 0)

        tab2_w = tile("tab2_w", [P, T2], U16)
        wp_raw = [tile(f"wp_raw{g}", [P, 2, KPASS], U16) for g in range(GROUPS)]
        tab_w = [tile(f"tab_w{a}", [P, T1], I32) for a in range(2)]
        w3_raw = [tile(f"w3_raw{a}", [P, H], I32) for a in range(2)]
        wv_raw = [[tile(f"wv_raw{g}{u}", [P, PACK, 256], F32) for u in range(2)] for g in range(GROUPS)]
        gain_sb = tile("gain_sb", [P, GROUPS, PACK], F32)
        wv_rows = wv.rearrange("(p i) c -> p i c", i=PACK)

        def load_wv(g, u):
            c0 = KPASS * g + 256 * u
            nc.sync.dma_start(out=wv_raw[g][u][:], in_=wv_rows[:, :, c0 : c0 + 256])

        def load_scales(queue, plane, first_row, scales):
            rows = scales.shape[0] * 4
            for q in range(4):
                queue.dma_start(
                    out=plane[32 * q + first_row : 32 * q + first_row + rows, :].bitcast(I32),
                    in_=scales.bitcast(I32)[:, 4 * q : 4 * q + 4, :],
                )

        v2_w = tile("v2_w", [P, S], U16)
        v2_s = tile("v2_s", [P, S], U8)
        v_s = tile("v_s", [P, S], U8)
        v_w = [tile(f"v_w{a}", [P, S], U32) for a in range(2)]

        def load_wp(g):
            pairs = wp_words.bitcast(I32).rearrange("a p c -> p a c")
            nc.sync.dma_start(out=wp_raw[g][:].bitcast(I32), in_=pairs[:, :, 256 * g : 256 * (g + 1)])

        def load_tab(a):
            nc.sync.dma_start(out=tab_w[a][:], in_=tab_words[a].rearrange("p t i -> p (t i)").bitcast(I32))

        nc.sync.dma_start(idx2[:], offs2)
        nc.sync.dma_start(out=tab2_w[:].bitcast(I32), in_=tab2_words[0].bitcast(I32))
        nc.sync.dma_start(idx[:], offs)
        for r in range(4):
            nc.scalar.dma_start(
                out=tab_s[r:P:16, :].bitcast(I32),
                in_=tab_scales.bitcast(I32)[:, r:16:4, :].rearrange("a q c -> q a c"),
            )
        load_scales(nc.gpsimd, w_s_raw[:, 1, :], 4, w3_scales)
        nc.gpsimd.dma_start(out=gain_sb[:], in_=gain.rearrange("(g p t) -> p g t", g=GROUPS, t=PACK))
        load_wv(0, 0)
        load_wv(0, 1)
        load_wp(0)
        for r in range(4):
            nc.sync.dma_start(out=tab2_s[r:P:32, :].bitcast(I32), in_=tab2_scales.bitcast(I32)[0, r:16:4, :])
        load_tab(0)
        nc.vector.tensor_copy(v2_w[:], tab2_w[:].indirect(idx2[:]))
        nc.vector.tensor_copy(v_s[:], tab_s[:].indirect(idx[:]))
        for r in range(4):
            nc.sync.dma_start(
                out=w_s_raw[r:P:32, :, :].bitcast(I32),
                in_=wp_scales.bitcast(I32)[:, r:16:4, :].rearrange("a q c -> q a c"),
            )
        load_tab(1)
        nc.sync.dma_start(out=v_s1[0 : P - 16, :].bitcast(I32), in_=v_s[16:P, :].bitcast(I32))
        load_wp(1)
        load_wv(1, 0)
        load_wv(1, 1)
        for a in range(2):
            nc.sync.dma_start(out=w3_raw[a][:], in_=w3_words[a].rearrange("p c i -> p (c i)").bitcast(I32))

        w_s = [tile(f"w_s{a}", [P, H], U8) for a in range(2)]

        def deal_scales(a):
            (nc.vector, nc.gpsimd)[a].tensor_copy(
                out=w_s[a][:].rearrange("p (g t c i) -> p g c t i", g=GROUPS, t=PACK, i=16),
                in_=w_s_raw[:, a, :].rearrange("p (g c i t) -> p g c t i", g=GROUPS, t=PACK, i=16),
            )

        wp_w = [tile(f"wp_w{g}", [P, 2, KPASS], U16) for g in range(GROUPS)]

        def deal_wp(g):
            nc.vector.tensor_copy(
                out=wp_w[g][:].rearrange("p a (u e m) -> p a u m e", u=2, e=2),
                in_=wp_raw[g][:].rearrange("p a (m u e) -> p a u m e", u=2, e=2),
            )

        nwv_w = [tile(f"nwv_w{g}", [P, KPASS], U32) for g in range(GROUPS)]
        nwv_s = [tile(f"nwv_s{g}", [P, KPASS], U8) for g in range(GROUPS)]

        def quantise_wv(g):
            nwv_b = tile(f"nwv_b{g}", [P, PACK, P, PACK], BF16)
            for u in range(2):
                nc.scalar.activation(
                    out=nwv_b[:, :, 64 * u : 64 * (u + 1), :].rearrange("p t m i -> p m i t"),
                    in_=wv_raw[g][u][:].rearrange("p i (m t) -> p m i t", t=PACK),
                    func=ACT.Copy,
                    scale=-1.0,
                )
            for t0 in (0, 2):
                cols = slice(P * t0, P * (t0 + 2))
                nc.vector.quantize_mx(
                    out=nwv_w[g][:, cols].bitcast(FP8X4),
                    scales=nwv_s[g][:, cols],
                    in_=nwv_b[:, t0 : t0 + 2, :, :].rearrange("p t m i -> p (t m i)"),
                )

        def plant_pass(bank, g, t, a, bays, start, stop):
            cols = slice(P * t, P * (t + 1))
            wide = slice(KPASS * g + P * t, KPASS * g + P * (t + 1))
            nc.tensor.matmul_mx(
                out=bank,
                lhsT=wp_w[g][:, a, cols].bitcast(FP4X4),
                lhsT_scale=w_s[a][:, wide],
                rhs=v_w[a][:, bays].bitcast(FP8X4),
                rhs_scale=(v_s, v_s1)[a][:, bays],
                start=start,
                stop=stop,
            )

        def vent_pass(bank, g, t, bays, start, stop=True):
            cols = slice(P * t, P * (t + 1))
            nc.tensor.matmul_mx(
                out=bank,
                lhsT=nwv_w[g][:, cols].bitcast(FP8X4),
                lhsT_scale=nwv_s[g][:, cols],
                rhs=v2_w[:, bays].bitcast(FP4X4),
                rhs_scale=v2_s[:, bays],
                start=start,
                stop=stop,
            )

        all_bays = slice(0, S)
        deal_wp(0)
        nc.vector.tensor_copy(v2_s[:], tab2_s[:].indirect(idx2[:]))
        quantise_wv(0)
        nb0 = tile("nb0", [P, PACK, S], F32)
        d0 = tile("d0", [P, PACK, S], F32, tag="wp_raw1")
        for t in range(PACK):
            bank = bank_tile(t, [P, S])
            vent_pass(bank[:], 0, t, all_bays, True)
            nc.scalar.copy(out=nb0[:, t, :], in_=bank[:])
        nc.vector.tensor_copy(v_w[0][:], tab_w[0][:].bitcast(U32).indirect(idx[:]))
        deal_scales(0)
        a_banks = [bank_tile(PACK + t, [P, S]) for t in range(PACK)]
        for t in range(PACK):
            plant_pass(a_banks[t][:], 0, t, 0, all_bays, True, False)
        deal_scales(1)
        nc.vector.tensor_copy(v_w[1][:], tab_w[1][:].bitcast(U32).indirect(idx[:]))
        for t in range(PACK):
            plant_pass(a_banks[t][:], 0, t, 1, all_bays, False, True)
        deal_wp(1)
        quantise_wv(1)
        d1 = {}

        def difference(first, width):
            bays = slice(first, first + width)
            per_bank = KPASS // width
            for t0 in range(0, PACK, per_bank):
                bank = bank_tile(first // P + t0 // per_bank, [P, per_bank, width])
                d1[first, t0] = bank
                products = ("vent", 1, 0) if first + width == S else (1, 0, "vent")
                for k, a in enumerate(products):
                    for s in range(per_bank):
                        start, stop = (k, s) == (0, 0), (k, s) == (2, per_bank - 1)
                        if a == "vent":
                            vent_pass(bank[:, s, :], 1, t0 + s, bays, start, stop)
                        else:
                            plant_pass(bank[:, s, :], 1, t0 + s, a, bays, start, stop)

        head, middle, last = CHUNKS
        difference(*head)
        difference(*middle)
        for t in range(PACK):
            nc.vector.tensor_tensor(out=d0[:, t, :], in0=a_banks[t][:], in1=nb0[:, t, :], op=ALU.add)

        w3_w = [tile(f"w3_w{a}", [P, H], I32) for a in range(2)]
        for a in range(2):
            nc.vector.tensor_copy(
                out=w3_w[a][:].rearrange("p (g u e m) -> p g u m e", g=GROUPS, u=2, e=2),
                in_=w3_raw[a][:].rearrange("p (g m u e) -> p g u m e", g=GROUPS, u=2, e=2),
            )

        z0_rows = tile("z0_rows", [P, PACK * S], BF16, tag="wv_raw11")

        z = {}

        z_rows = {}

        def scale_z(g, first, width):
            bays = slice(first, first + width)
            if g == 0:
                rows = z0_rows[:, PACK * first : PACK * (first + width)].rearrange("p (t j) -> p t j", t=PACK)
            else:
                rows = tile(f"z_rows{g}_{first}", [P, PACK, width], BF16)[:]
            for t in range(PACK):
                per_bank = KPASS // width
                d_rows = d0[:, t, bays] if g == 0 else d1[first, t - t % per_bank][:, t % per_bank, :]
                nc.scalar.activation(out=rows[:, t, :], in_=d_rows, func=ACT.Copy, scale=gain_sb[:, g, t : t + 1])
            z_rows[g, first] = rows

        def quantise_z(g, first, width, weave, tag=None):
            z_b = tile(f"z_b{g}_{first}", [P, width, PACK], BF16, tag=tag)
            z_w = tile(f"z_w{g}_{first}", [P, width], U32)
            z_s = tile(f"z_s{g}_{first}", [P, width], U8)
            if weave is None:
                nc.vector.tensor_tensor(
                    out=z_b[:].rearrange("p (c i) t -> p c t i", i=2),
                    in0=d1[first, 0][:].rearrange("p t (c i) -> p c t i", i=2),
                    in1=gain_sb[:, 1, :].unsqueeze(1).unsqueeze(3).to_broadcast([P, width // 2, PACK, 2]),
                    op=ALU.mult,
                )
            else:
                weave(
                    out=z_b[:].rearrange("p (c i) t -> p c t i", i=4),
                    in_=z_rows[g, first].rearrange("p t (c i) -> p c t i", i=4),
                )
            nc.vector.quantize_mx(out=z_w[:].bitcast(FP8X4), scales=z_s[:], in_=z_b[:].rearrange("p j t -> p (j t)"))
            z[g, first] = (z_w, z_s)

        y_s = tile("y_s", [P, GROUPS, S], U8)
        out_rows = out_0.rearrange("(g p t) j -> g p t j", g=GROUPS, t=PACK)
        gates, results = {}, {}

        def gate(first, width):
            per_bank = KPASS // width
            th = [tile(f"th{g}_{first}", [P, PACK, width], F32) for g in range(GROUPS)]
            gates[first] = th
            numbers = list({0: (4, 5), 128: (7, 4, 5, 0), 384: (4, 5)}[first])
            for g in (1, 0):
                for t0 in range(0, PACK, per_bank):
                    bank = bank_tile(numbers.pop(0), [P, per_bank, width])
                    for a in range(2):
                        for s in range(per_bank):
                            cols = slice(KPASS * g + P * (t0 + s), KPASS * g + P * (t0 + s + 1))
                            nc.tensor.matmul_mx(
                                out=bank[:, s, :],
                                lhsT=w3_w[a][:, cols].bitcast(FP8X4),
                                lhsT_scale=w_s[1][4 + 4 * a : P, cols],
                                rhs=z[a, first][0][:].bitcast(FP8X4),
                                rhs_scale=z[a, first][1][:],
                                start=(a, s) == (0, 0),
                                stop=(a, s) == (1, per_bank - 1),
                            )
                    nc.scalar.activation(out=th[g][:, t0 : t0 + per_bank, :], in_=bank[:], func=ACT.Tanh, scale=0.5)

        def mix(first, width):
            bays = slice(first, first + width)
            per_bank = KPASS // width
            th = gates[first]
            nb1 = {}
            for t0 in range(0, PACK, per_bank):
                nb1[t0] = bank_tile({0: (6,), 128: (6, 7), 384: (1,)}[first][t0 // per_bank], [P, per_bank, width])
                for s in range(per_bank):
                    vent_pass(nb1[t0][:, s, :], 1, t0 + s, bays, True)

            gd = [tile(f"gd{g}_{first}", [P, PACK, width], F32) for g in range(GROUPS)]
            y = [tile(f"y{g}_{first}", [P, PACK, width], F32) for g in range(GROUPS)]
            for t0 in range(0, PACK, per_bank):
                nc.vector.scalar_tensor_tensor(
                    out=gd[1][:, t0 : t0 + per_bank, :], in0=th[1][:, t0 : t0 + per_bank, :], scalar=1.0,
                    in1=d1[first, t0][:], op0=ALU.add, op1=ALU.mult,
                )
            nc.vector.scalar_tensor_tensor(
                out=gd[0][:], in0=th[0][:], scalar=1.0, in1=d0[:, :, bays], op0=ALU.add, op1=ALU.mult
            )
            for t0 in range(0, PACK, per_bank):
                nc.vector.scalar_tensor_tensor(
                    out=y[1][:, t0 : t0 + per_bank, :], in0=gd[1][:, t0 : t0 + per_bank, :], scalar=0.5,
                    in1=nb1[t0][:], op0=ALU.mult, op1=ALU.subtract,
                )
            halves = 2 if first + width == S else 1
            for h in range(halves):
                part = slice(width // halves * h, width // halves * (h + 1))
                nc.vector.scalar_tensor_tensor(
                    out=y[0][:, :, part], in0=gd[0][:, :, part], scalar=0.5,
                    in1=nb0[:, :, first + part.start : first + part.stop], op0=ALU.mult, op1=ALU.subtract,
                )
            results[first] = y

        rounded_y = {}

        def round_y(first, width):
            bays = slice(first, first + width)
            y = results[first]
            for g in (1, 0):
                nc.sync.dma_start(out=out_rows[g][:, :, bays], in_=y[g][:])
                y_b = tile(f"y_b{g}_{first}", [P, width, PACK], BF16)
                halves = 2 if g == 0 and first + width == S else 1
                for h in range(halves):
                    part = slice(width // halves * h, width // halves * (h + 1))
                    nc.scalar.copy(
                        out=y_b[:, part, :].rearrange("p (c i) t -> p c t i", i=2),
                        in_=y[g][:, :, part].rearrange("p t (c i) -> p c t i", i=2),
                    )
                rounded_y[g, first] = y_b

        def quantise_y(first, width):
            bays = slice(first, first + width)
            y_w = tile(f"y_w{first}", [P, GROUPS, width], U32)
            for g in (1, 0):
                nc.vector.quantize_mx(
                    out=y_w[:, g, :].bitcast(FP8X4),
                    scales=y_s[:, g, bays],
                    in_=rounded_y[g, first][:].rearrange("p j t -> p (j t)"),
                )
            nc.sync.dma_start(
                out=out_1[:, :, bays, :].rearrange("g p j t -> p g (j t)").bitcast(I32), in_=y_w[:].bitcast(I32)
            )

        quantise_z(1, *head, None)
        scale_z(0, *head)
        quantise_z(0, *head, nc.vector.tensor_copy)
        for g in (1, 0):
            scale_z(g, *middle)
            quantise_z(g, *middle, nc.vector.tensor_copy)
        gate(*head)
        difference(*last)
        for g in (1, 0):
            scale_z(g, *last)
        mix(*head)
        for g in (1, 0):
            quantise_z(g, *last, nc.scalar.copy, f"z_w{g}_0")
        gate(*middle)
        round_y(*head)
        quantise_y(*head)
        mix(*middle)
        gate(*last)
        round_y(*middle)
        mix(*last)
        round_y(*last)
        quantise_y(*middle)
        quantise_y(*last)
        for q in range(4):
            (nc.scalar, nc.sync, nc.scalar, nc.sync)[q].dma_start(
                out=out_2[:, 4 * q : 4 * q + 4, :].rearrange("g r j -> r g j").bitcast(I32),
                in_=y_s[32 * q : 32 * q + 4, :, :].bitcast(I32),
            )
